import numpy as np
import ml_dtypes


def mxq(x, axis, fmt="e4m3"):
    dtype, down = {"e4m3": (ml_dtypes.float8_e4m3fn, 7), "e5m2": (ml_dtypes.float8_e5m2, 14)}[fmt]
    v = np.moveaxis(np.asarray(x, np.float32).astype(ml_dtypes.bfloat16).astype(np.float64), axis, -1)
    blocks = v.reshape(v.shape[:-1] + (-1, 32))
    amax = np.abs(blocks).max(-1, keepdims=True)
    byte = np.maximum(np.where(amax > 0, np.frexp(amax)[1] - 1 + 127, 0) - down, 1)
    scale = np.exp2(byte - 127.0)
    codes = (blocks / scale).astype(np.float32).astype(dtype).astype(np.float64)
    return np.moveaxis((codes * scale).reshape(v.shape), -1, axis)


WIDE = False


def mx_kscale(k):
    if not WIDE:
        return np.ones(k)
    levels = np.array([10, -10, 5, -5, 0])
    if k % 512:
        return np.exp2(np.random.permutation(np.resize(levels, k // 32))).repeat(32)
    a = np.empty((k // 512, 16))
    for p in range(k // 512):
        a[p, :8] = np.random.permutation(np.resize(levels, 8))
        for g in range(8):
            far = levels[np.abs(levels - a[p, g]) >= 10]
            a[p, g + 8] = far[np.random.randint(len(far))]
    return np.exp2(a.ravel()).repeat(32)


def f64(x):
    return np.asarray(x).astype(np.float64)


E2M1 = np.array([0.0, 0.5, 1.0, 1.5, 2.0, 3.0, 4.0, 6.0, -0.0, -0.5, -1.0, -1.5, -2.0, -3.0, -4.0, -6.0])


def pack_weight(w, fmt):
    k, n = w.shape
    w = f64(np.asarray(w, np.float32).astype(ml_dtypes.bfloat16)).reshape(k // 32, 32, n)
    amax = np.abs(w).max(1)
    if fmt == "e4m3":
        byte = np.frexp(amax)[1] - 1 + 127 - 7
    else:
        mant, ex = np.frexp(amax / 6.0)
        byte = np.where(mant > 0.5, ex, ex - 1) + 127
    byte = np.clip(np.where(amax > 0, byte, 1), 1, 254)
    scaled = (w * np.exp2(127.0 - byte)[:, None, :]).reshape(k, n).astype(np.float32)
    by_word = np.ascontiguousarray(scaled.reshape(k // 512, 128, 4, n).transpose(0, 1, 3, 2))
    if fmt == "e4m3":
        words = by_word.astype(ml_dtypes.float8_e4m3fn).view(np.uint8)
    else:
        c = by_word.astype(ml_dtypes.float4_e2m1fn).view(np.uint8) & 0xF
        words = (c[..., 0::2] | (c[..., 1::2] << 4)).reshape(k // 512, 128, 2 * n)
    return np.ascontiguousarray(words), np.ascontiguousarray(byte.astype(np.uint8).reshape(k // 512, 16, n))


def unpack_weight(words, scales, fmt):
    g, _, n = scales.shape
    words = np.ascontiguousarray(words).reshape(g, 128, n, -1)
    if fmt == "e4m3":
        vals = words.view(ml_dtypes.float8_e4m3fn).astype(np.float64)
    else:
        nib = np.empty((g, 128, n, 4), np.uint8)
        nib[..., 0::2] = words & 0xF
        nib[..., 1::2] = words >> 4
        vals = E2M1[nib]
    vals = vals * np.repeat(np.exp2(scales.astype(np.float64) - 127.0), 8, axis=1)[..., None]
    return vals.transpose(0, 1, 3, 2).reshape(g * 512, n)


def bf(x):
    return np.asarray(x, np.float32).astype(ml_dtypes.bfloat16)


def planes(Y):
    r, m = Y.shape
    b = f64(bf(Y)).reshape(r // 32, 32, m)
    amax = np.abs(b).max(1)
    byte = np.clip(np.where(amax > 0, np.frexp(amax)[1] - 1 + 127 - 7, 1), 1, 254)
    codes = (b * np.exp2(127.0 - byte)[:, None, :]).reshape(r, m).astype(np.float32).astype(ml_dtypes.float8_e4m3fn).view(np.uint8)
    words = codes.reshape(r // 512, 128, 4, m).transpose(0, 1, 3, 2)
    return np.ascontiguousarray(words), np.ascontiguousarray(byte.astype(np.uint8).reshape(r // 512, 16, m))


K, L, T, N = 1024, 512, 512, 512


def setup_inputs():
    n = np.random.standard_normal
    fk = mx_kscale(K)
    fl = mx_kscale(L)
    wap = pack_weight(n((K, N)) * 1 / np.sqrt(K) * fk[:, None], "e2m1")
    xqp = pack_weight(n((L, T)) * 0.5 / fl[:, None], "e4m3")
    wsp = pack_weight(n((L, N)) * 1 / np.sqrt(L) * fl[:, None], "e2m1")
    wvp = pack_weight(n((K, N)) * 1 / np.sqrt(K) * fk[:, None], "e4m3")
    return {
        "xt": (n((K, T)) * 0.7 / fk[:, None]).astype(np.float32),
        "wa_words": wap[0],
        "wa_scales": wap[1],
        "xq_words": xqp[0],
        "xq_scales": xqp[1],
        "ws_words": wsp[0],
        "ws_scales": wsp[1],
        "wv_words": wvp[0],
        "wv_scales": wvp[1],
        "bi": (np.random.uniform(-0.5, 0.5, (1, N))).astype(np.float32),
    }


def reference(xt, wa_words, wa_scales, xq_words, xq_scales, ws_words, ws_scales, wv_words, wv_scales, bi):
    wau = unpack_weight(wa_words, wa_scales, "e2m1")
    xqu = unpack_weight(xq_words, xq_scales, "e4m3")
    wsu = unpack_weight(ws_words, ws_scales, "e2m1")
    wvu = unpack_weight(wv_words, wv_scales, "e4m3")
    xtq = mxq(f64(xt), 0, "e4m3")
    a = xtq.T @ wau + xqu.T @ wsu
    v = xtq.T @ wvu
    e = np.exp(a)
    y = 512.0 * e / np.sum(e, axis=1, keepdims=True) * (v + f64(bi))
    words, scales = planes(y)
    return y, words, scales

@@ -1,0 +1,236 @@
+from contextlib import ExitStack
+
+import concourse.mybir as mybir
+from concourse.masks import make_identity
+
+K, L, T, N = 1024, 512, 512, 512
+FLOPS = 2 * T * N * (K + L + K)
+
+F32 = mybir.dt.float32
+BF16 = mybir.dt.bfloat16
+I32 = mybir.dt.int32
+U32 = mybir.dt.uint32
+U8 = mybir.dt.uint8
+FP8X4 = mybir.dt.float8_e4m3fn_x4
+FP4X4 = mybir.dt.float4_e2m1fn_x4
+ALU = mybir.AluOpType
+ACT = mybir.ActivationFunctionType
+
+P = 128
+PACK = 4
+K_PASS = P * PACK
+BANK = 512
+QUADS = 4
+HALF = T // 2
+SHARE = 512.0
+
+CHUNKS = ((0, 256), (256, 128), (384, 128))
+VEC_M_PASS0 = 80
+VEC_M_HALF = (32, 40)
+VEC_COLS_LAST = 80
+
+
+def load_scales(nc, plane, scales):
+    for q in range(QUADS):
+        nc.sync.dma_start(
+            out=plane[32 * q : 32 * q + 4, :, :].bitcast(I32),
+            in_=scales[:, 4 * q : 4 * q + 4, :].rearrange("z q n -> q z n").bitcast(I32),
+        )
+
+
+def deal_and_round(nc, grouped, raw, vec_m):
+    count = grouped.shape[2]
+    dst = grouped.rearrange("p r m j -> p m j r")
+    src = raw.rearrange("p j (m r) -> p m j r", r=PACK)
+    nc.vector.tensor_copy(out=dst[:, :vec_m], in_=src[:, :vec_m])
+    nc.scalar.copy(out=dst[:, vec_m:count], in_=src[:, vec_m:count])
+
+
+def tile_mix_features_share_a_gate_pl_kernel(
+    tc, xt, wa_words, wa_scales, xq_words, xq_scales, ws_words, ws_scales, wv_words, wv_scales, bi,
+    out_0, out_1, out_2,
+):
+    nc = tc.nc
+    with ExitStack() as ctx:
+        sb = ctx.enter_context(tc.tile_pool(name="sb", bufs=1))
+        ps = ctx.enter_context(tc.psum_pool(name="ps", bufs=1))
+        ctx.enter_context(tc.manual_schedule())
+
+        xq_sc_raw = sb.tile([P, 1, T], U8, align_bytes=64)
+        ws_sc = sb.tile([P, 1, N], U8, align_bytes=64)
+        wa_sc = sb.tile([P, 2, N], U8, align_bytes=64)
+        wv_sc = sb.tile([P, 2, N], U8, align_bytes=64)
+        nc.gpsimd.memset(xq_sc_raw[:].bitcast(U32), 0)
+        for plane in (ws_sc, wa_sc, wv_sc):
+            nc.vector.memset(plane[:].bitcast(U32), 0)
+
+        b_cols = sb.tile([P, PACK], F32)
+        nc.scalar.dma_start(out=b_cols[:], in_=bi.rearrange("o (k j) -> k (o j)", j=PACK))
+        warm = sb.tile([P, 8], F32)
+        nc.vector.memset(warm[:, 0:4], 0.0)
+        nc.scalar.activation(out=warm[:, 4:5], in_=warm[:, 0:1], func=ACT.Exp)
+
+        ident = sb.tile([P, P], F32)
+        make_identity(nc, ident[:])
+
+        xq_raw = sb.tile([P, T], I32, align_bytes=64)
+        x0_raw = sb.tile([P, PACK, T], F32, align_bytes=64)
+        x1_raw = [sb.tile([P, PACK, HALF], F32, align_bytes=64, name=f"x1_raw{h}") for h in range(2)]
+        ws = sb.tile([P, 2 * N], U8, align_bytes=64)
+        wa = sb.tile([P, 2, 2 * N], U8, align_bytes=64)
+        wv = sb.tile([P, 2, N], U32, align_bytes=64)
+        xt_rows = xt.rearrange("(z p j) t -> z p j t", p=P, j=PACK)
+
+        nc.sync.dma_start(out=xq_raw[:], in_=xq_words.rearrange("z p c t -> p (z c t)").bitcast(I32))
+        load_scales(nc, xq_sc_raw, xq_scales)
+        nc.sync.dma_start(out=x0_raw[:], in_=xt_rows[0])
+        nc.sync.dma_start(out=ws[:].bitcast(I32), in_=ws_words.rearrange("z p b -> p (z b)").bitcast(I32))
+        nc.sync.dma_start(out=x1_raw[0][:], in_=xt_rows[1][:, :, :HALF])
+        load_scales(nc, ws_sc, ws_scales)
+        nc.sync.dma_start(out=x1_raw[1][:], in_=xt_rows[1][:, :, HALF:])
+        load_scales(nc, wa_sc, wa_scales)
+        nc.sync.dma_start(out=wa[:].bitcast(I32), in_=wa_words.rearrange("z p b -> p z b").bitcast(I32))
+        load_scales(nc, wv_sc, wv_scales)
+        nc.sync.dma_start(out=wv[:].bitcast(I32), in_=wv_words.rearrange("z p n t -> p z (n t)").bitcast(I32))
+
+        xq = sb.tile([P, T], I32, align_bytes=64)
+        xq_sc = sb.tile([P, T], U8, align_bytes=64)
+        nc.vector.tensor_copy(
+            out=xq[:].rearrange("p (r m) -> p m r", r=PACK), in_=xq_raw[:].rearrange("p (m r) -> p m r", r=PACK)
+        )
+        nc.vector.tensor_copy(
+            out=xq_sc[:].rearrange("p (r m) -> p m r", r=PACK),
+            in_=xq_sc_raw[:, 0, :].rearrange("p (m r) -> p m r", r=PACK),
+        )
+
+        b_bank = ps.tile([P, PACK, P], F32, tag="v3")
+        for j in range(PACK):
+            nc.tensor.transpose(b_bank[:, j, :], b_cols[:, j : j + 1].to_broadcast([P, P]), ident[:])
+        b_rows = sb.tile([P, N], F32)
+        nc.vector.tensor_scalar(
+            out=b_rows[:].rearrange("p (k j) -> p k j", j=PACK),
+            in0=b_bank[:].rearrange("p j k -> p k j"),
+            scalar1=SHARE, scalar2=None, op0=ALU.mult,
+        )
+
+        x_codes = [sb.tile([P, T], U32, align_bytes=64, name=f"x_codes{z}") for z in range(2)]
+        x_sc = [sb.tile([P, T], U8, align_bytes=64, name=f"x_sc{z}") for z in range(2)]
+        g0 = sb.tile([P, PACK, P, PACK], BF16, align_bytes=64)
+        deal_and_round(nc, g0[:], x0_raw[:], VEC_M_PASS0)
+        nc.vector.quantize_mx(
+            out=x_codes[0][:].bitcast(FP8X4), scales=x_sc[0][:], in_=g0[:].rearrange("p r m j -> p (r m j)")
+        )
+        for h in range(2):
+            g1 = sb.tile([P, PACK, P // 2, PACK], BF16, align_bytes=64, name=f"g1{h}")
+            deal_and_round(nc, g1[:], x1_raw[h][:], VEC_M_HALF[h])
+            for r in range(PACK):
+                cols = slice(r * P + h * P // 2, r * P + (h + 1) * P // 2)
+                nc.vector.quantize_mx(
+                    out=x_codes[1][:, cols].bitcast(FP8X4),
+                    scales=x_sc[1][:, cols],
+                    in_=g1[:, r].rearrange("p m j -> p (m j)"),
+                )
+
+        gate = [ps.tile([P, BANK], F32, tag=f"a{r}", name=f"gate{r}") for r in range(PACK)]
+
+        def gate_pass(r, z):
+            toks = slice(r * P, (r + 1) * P)
+            nc.tensor.matmul_mx(
+                out=gate[r][:], lhsT=x_codes[z][:, toks].bitcast(FP8X4), lhsT_scale=x_sc[z][:, toks],
+                rhs=wa[:, z, :].bitcast(FP4X4), rhs_scale=wa_sc[:, z, :], start=False, stop=(z == 1),
+            )
+
+        for r in range(PACK):
+            toks = slice(r * P, (r + 1) * P)
+            nc.tensor.matmul_mx(
+                out=gate[r][:], lhsT=xq[:, toks].bitcast(FP8X4), lhsT_scale=xq_sc[:, toks],
+                rhs=ws[:].bitcast(FP4X4), rhs_scale=ws_sc[:, 0, :], start=True, stop=False,
+            )
+        for r, z in ((0, 0), (1, 0), (0, 1), (1, 1), (2, 0), (2, 1), (3, 0), (3, 1)):
+            gate_pass(r, z)
+
+        neg_max = sb.tile([P, PACK], F32)
+        sums = sb.tile([P, PACK], F32)
+        inv = sb.tile([P, PACK], F32)
+        e = [sb.tile([P, N], F32, name=f"e{r}") for r in range(PACK)]
+        for r in range(PACK):
+            nc.vector.tensor_reduce(
+                out=neg_max[:, r : r + 1], in_=gate[r][:], axis=mybir.AxisListType.X, op=ALU.max, negate=True
+            )
+            nc.scalar.activation(
+                out=e[r][:], in_=gate[r][:], func=ACT.Exp, bias=neg_max[:, r : r + 1], scale=1.0,
+                accum_out=sums[:, r : r + 1],
+            )
+
+        y_rows = out_0.rearrange("(p r) n -> p r n", r=PACK)
+        word_rows = out_1.rearrange("z p c t -> p (z c t)").bitcast(I32)
+        y_sc = sb.tile([P, N], U8, align_bytes=64)
+        vb = {}
+        y = {}
+        yg = {}
+        bank_no = [0]
+
+        def values(c):
+            c0, w = CHUNKS[c]
+            vb[c] = sb.tile([P, PACK, w], F32, name=f"vb{c}")
+            per_bank = BANK // w
+            for r0 in range(0, PACK, per_bank):
+                bank = ps.tile([P, per_bank, w], F32, tag=f"v{bank_no[0]}", name=f"val{bank_no[0]}")
+                bank_no[0] = bank_no[0] + 1
+                for r in range(r0, r0 + per_bank):
+                    toks = slice(r * P, (r + 1) * P)
+                    for z in range(2):
+                        nc.tensor.matmul_mx(
+                            out=bank[:, r - r0, :], lhsT=x_codes[z][:, toks].bitcast(FP8X4),
+                            lhsT_scale=x_sc[z][:, toks],
+                            rhs=wv[:, z, c0 : c0 + w].bitcast(FP8X4), rhs_scale=wv_sc[:, z, c0 : c0 + w],
+                            start=(z == 0), stop=(z == 1),
+                        )
+                nc.vector.scalar_tensor_tensor(
+                    out=vb[c][:, r0 : r0 + per_bank, :], in0=bank[:], scalar=SHARE,
+                    in1=b_rows[:, c0 : c0 + w].unsqueeze(1).to_broadcast([P, per_bank, w]),
+                    op0=ALU.mult, op1=ALU.add,
+                )
+
+        def products(c, vec_cols):
+            c0, w = CHUNKS[c]
+            y[c] = sb.tile([P, PACK, w], F32, name=f"y{c}")
+            yg[c] = sb.tile([P, w, PACK], BF16, align_bytes=64, name=f"yg{c}")
+            for r in range(PACK):
+                nc.vector.scalar_tensor_tensor(
+                    out=y[c][:, r, :], in0=e[r][:, c0 : c0 + w], scalar=inv[:, r : r + 1], in1=vb[c][:, r, :],
+                    op0=ALU.mult, op1=ALU.mult,
+                )
+            nc.sync.dma_start(out=y_rows[:, :, c0 : c0 + w], in_=y[c][:])
+            nc.scalar.copy(
+                out=yg[c][:, vec_cols:, :].rearrange("p (c i) r -> p c r i", i=PACK),
+                in_=y[c][:, :, vec_cols:].rearrange("p r (c i) -> p c r i", i=PACK),
+            )
+
+        def planes(c):
+            c0, w = CHUNKS[c]
+            words = sb.tile([P, w], U32, align_bytes=64, name=f"words{c}")
+            nc.vector.quantize_mx(
+                out=words[:].bitcast(FP8X4), scales=y_sc[:, c0 : c0 + w], in_=yg[c][:].rearrange("p c r -> p (c r)")
+            )
+            nc.sync.dma_start(out=word_rows[:, c0 : c0 + w], in_=words[:].bitcast(I32))
+
+        values(0)
+        nc.vector.reciprocal(out=inv[:], in_=sums[:])
+        values(1)
+        products(0, 0)
+        values(2)
+        products(1, 0)
+        planes(0)
+        products(2, VEC_COLS_LAST)
+        planes(1)
+        nc.vector.tensor_copy(
+            out=yg[2][:, :VEC_COLS_LAST, :].rearrange("p (c i) r -> p c r i", i=PACK),
+            in_=y[2][:, :, :VEC_COLS_LAST].rearrange("p r (c i) -> p c r i", i=PACK),
+        )
+        planes(2)
+        for q in range(QUADS):
+            queue = nc.scalar if q % 2 else nc.sync
+            queue.dma_start(
+                out=out_2[0, 4 * q : 4 * q + 4, :].bitcast(I32), in_=y_sc[32 * q : 32 * q + 4, :].bitcast(I32)
+            )

@@ -26,13 +26,13 @@ SHARE = 512.0
 
 CHUNKS = ((0, 256), (256, 128), (384, 128))
 VEC_M_PASS0 = 80
-VEC_M_HALF = (32, 40)
-VEC_COLS_LAST = 80
+VEC_M_HALF = (72, 84)
+VEC_COLS_LAST = 224
 
 
-def load_scales(nc, plane, scales):
+def load_scales(queue, plane, scales):
     for q in range(QUADS):
-        nc.sync.dma_start(
+        queue.dma_start(
             out=plane[32 * q : 32 * q + 4, :, :].bitcast(I32),
             in_=scales[:, 4 * q : 4 * q + 4, :].rearrange("z q n -> q z n").bitcast(I32),
         )
@@ -66,32 +66,29 @@ def tile_mix_features_share_a_gate_pl_kernel(
 
         b_cols = sb.tile([P, PACK], F32)
         nc.scalar.dma_start(out=b_cols[:], in_=bi.rearrange("o (k j) -> k (o j)", j=PACK))
-        warm = sb.tile([P, 8], F32)
-        nc.vector.memset(warm[:, 0:4], 0.0)
-        nc.scalar.activation(out=warm[:, 4:5], in_=warm[:, 0:1], func=ACT.Exp)
 
         ident = sb.tile([P, P], F32)
         make_identity(nc, ident[:])
 
         xq_raw = sb.tile([P, T], I32, align_bytes=64)
         x0_raw = sb.tile([P, PACK, T], F32, align_bytes=64)
-        x1_raw = [sb.tile([P, PACK, HALF], F32, align_bytes=64, name=f"x1_raw{h}") for h in range(2)]
+        x1_raw = [sb.tile([P, 2, T], F32, align_bytes=64, name=f"x1_raw{h}") for h in range(2)]
         ws = sb.tile([P, 2 * N], U8, align_bytes=64)
         wa = sb.tile([P, 2, 2 * N], U8, align_bytes=64)
         wv = sb.tile([P, 2, N], U32, align_bytes=64)
         xt_rows = xt.rearrange("(z p j) t -> z p j t", p=P, j=PACK)
 
         nc.sync.dma_start(out=xq_raw[:], in_=xq_words.rearrange("z p c t -> p (z c t)").bitcast(I32))
-        load_scales(nc, xq_sc_raw, xq_scales)
-        nc.sync.dma_start(out=x0_raw[:], in_=xt_rows[0])
         nc.sync.dma_start(out=ws[:].bitcast(I32), in_=ws_words.rearrange("z p b -> p (z b)").bitcast(I32))
-        nc.sync.dma_start(out=x1_raw[0][:], in_=xt_rows[1][:, :, :HALF])
-        load_scales(nc, ws_sc, ws_scales)
-        nc.sync.dma_start(out=x1_raw[1][:], in_=xt_rows[1][:, :, HALF:])
-        load_scales(nc, wa_sc, wa_scales)
+        load_scales(nc.sync, xq_sc_raw, xq_scales)
+        nc.sync.dma_start(out=x0_raw[:], in_=xt_rows[0])
+        load_scales(nc.sync, ws_sc, ws_scales)
+        nc.sync.dma_start(out=x1_raw[0][:], in_=xt_rows[1][:, 0:2, :])
+        nc.sync.dma_start(out=x1_raw[1][:], in_=xt_rows[1][:, 2:4, :])
+        load_scales(nc.sync, wa_sc, wa_scales)
         nc.sync.dma_start(out=wa[:].bitcast(I32), in_=wa_words.rearrange("z p b -> p z b").bitcast(I32))
-        load_scales(nc, wv_sc, wv_scales)
         nc.sync.dma_start(out=wv[:].bitcast(I32), in_=wv_words.rearrange("z p n t -> p z (n t)").bitcast(I32))
+        load_scales(nc.sync, wv_sc, wv_scales)
 
         xq = sb.tile([P, T], I32, align_bytes=64)
         xq_sc = sb.tile([P, T], U8, align_bytes=64)
@@ -107,11 +104,13 @@ def tile_mix_features_share_a_gate_pl_kernel(
         for j in range(PACK):
             nc.tensor.transpose(b_bank[:, j, :], b_cols[:, j : j + 1].to_broadcast([P, P]), ident[:])
         b_rows = sb.tile([P, N], F32)
-        nc.vector.tensor_scalar(
+        nc.scalar.activation(
             out=b_rows[:].rearrange("p (k j) -> p k j", j=PACK),
-            in0=b_bank[:].rearrange("p j k -> p k j"),
-            scalar1=SHARE, scalar2=None, op0=ALU.mult,
+            in_=b_bank[:].rearrange("p j k -> p k j"),
+            func=ACT.Copy, scale=SHARE,
         )
+
+        H = N // 2
 
         x_codes = [sb.tile([P, T], U32, align_bytes=64, name=f"x_codes{z}") for z in range(2)]
         x_sc = [sb.tile([P, T], U8, align_bytes=64, name=f"x_sc{z}") for z in range(2)]
@@ -120,16 +119,16 @@ def tile_mix_features_share_a_gate_pl_kernel(
         nc.vector.quantize_mx(
             out=x_codes[0][:].bitcast(FP8X4), scales=x_sc[0][:], in_=g0[:].rearrange("p r m j -> p (r m j)")
         )
+        g1 = sb.tile([P, PACK, P, PACK], BF16, align_bytes=64)
         for h in range(2):
-            g1 = sb.tile([P, PACK, P // 2, PACK], BF16, align_bytes=64, name=f"g1{h}")
-            deal_and_round(nc, g1[:], x1_raw[h][:], VEC_M_HALF[h])
-            for r in range(PACK):
-                cols = slice(r * P + h * P // 2, r * P + (h + 1) * P // 2)
-                nc.vector.quantize_mx(
-                    out=x_codes[1][:, cols].bitcast(FP8X4),
-                    scales=x_sc[1][:, cols],
-                    in_=g1[:, r].rearrange("p m j -> p (m j)"),
-                )
+            deal_and_round(nc, g1[:, :, :, 2 * h : 2 * h + 2], x1_raw[h][:], VEC_M_HALF[h])
+        for r in range(0, PACK, 2):
+            cols = slice(r * P, (r + 2) * P)
+            nc.vector.quantize_mx(
+                out=x_codes[1][:, cols].bitcast(FP8X4),
+                scales=x_sc[1][:, cols],
+                in_=g1[:, r : r + 2].rearrange("p r m j -> p (r m j)"),
+            )
 
         gate = [ps.tile([P, BANK], F32, tag=f"a{r}", name=f"gate{r}") for r in range(PACK)]
 
@@ -146,89 +145,108 @@ def tile_mix_features_share_a_gate_pl_kernel(
                 out=gate[r][:], lhsT=xq[:, toks].bitcast(FP8X4), lhsT_scale=xq_sc[:, toks],
                 rhs=ws[:].bitcast(FP4X4), rhs_scale=ws_sc[:, 0, :], start=True, stop=False,
             )
+        col_bank = ps.tile([P, 2, P], F32, tag="v2")
+        for q in range(2):
+            nc.tensor.transpose(col_bank[:, q, :], b_rows[:, H + q * P : H + (q + 1) * P], ident[:])
+        b_part = sb.tile([P, 2], F32)
+        nc.scalar.copy(out=b_part[:], in_=col_bank[:, :, 0])
         for r, z in ((0, 0), (1, 0), (0, 1), (1, 1), (2, 0), (2, 1), (3, 0), (3, 1)):
             gate_pass(r, z)
 
         neg_max = sb.tile([P, PACK], F32)
         sums = sb.tile([P, PACK], F32)
         inv = sb.tile([P, PACK], F32)
-        e = [sb.tile([P, N], F32, name=f"e{r}") for r in range(PACK)]
+        e = sb.tile([P, PACK, N], F32)
         for r in range(PACK):
             nc.vector.tensor_reduce(
                 out=neg_max[:, r : r + 1], in_=gate[r][:], axis=mybir.AxisListType.X, op=ALU.max, negate=True
             )
             nc.scalar.activation(
-                out=e[r][:], in_=gate[r][:], func=ACT.Exp, bias=neg_max[:, r : r + 1], scale=1.0,
+                out=e[:, r, :], in_=gate[r][:], func=ACT.Exp, bias=neg_max[:, r : r + 1], scale=1.0,
                 accum_out=sums[:, r : r + 1],
             )
 
         y_rows = out_0.rearrange("(p r) n -> p r n", r=PACK)
         word_rows = out_1.rearrange("z p c t -> p (z c t)").bitcast(I32)
         y_sc = sb.tile([P, N], U8, align_bytes=64)
-        vb = {}
-        y = {}
-        yg = {}
-        bank_no = [0]
+        y = sb.tile([P, PACK, N], F32)
 
-        def values(c):
-            c0, w = CHUNKS[c]
-            vb[c] = sb.tile([P, PACK, w], F32, name=f"vb{c}")
-            per_bank = BANK // w
-            for r0 in range(0, PACK, per_bank):
-                bank = ps.tile([P, per_bank, w], F32, tag=f"v{bank_no[0]}", name=f"val{bank_no[0]}")
-                bank_no[0] = bank_no[0] + 1
-                for r in range(r0, r0 + per_bank):
-                    toks = slice(r * P, (r + 1) * P)
-                    for z in range(2):
-                        nc.tensor.matmul_mx(
-                            out=bank[:, r - r0, :], lhsT=x_codes[z][:, toks].bitcast(FP8X4),
-                            lhsT_scale=x_sc[z][:, toks],
-                            rhs=wv[:, z, c0 : c0 + w].bitcast(FP8X4), rhs_scale=wv_sc[:, z, c0 : c0 + w],
-                            start=(z == 0), stop=(z == 1),
-                        )
-                nc.vector.scalar_tensor_tensor(
-                    out=vb[c][:, r0 : r0 + per_bank, :], in0=bank[:], scalar=SHARE,
-                    in1=b_rows[:, c0 : c0 + w].unsqueeze(1).to_broadcast([P, per_bank, w]),
-                    op0=ALU.mult, op1=ALU.add,
+        def values(name, rows, cols):
+            w = cols.stop - cols.start
+            bank = ps.tile([P, len(rows), w], F32, tag=name, name=f"val_{name}")
+            for i, r in enumerate(rows):
+                toks = slice(r * P, (r + 1) * P)
+                for z in range(2):
+                    nc.tensor.matmul_mx(
+                        out=bank[:, i, :], lhsT=x_codes[z][:, toks].bitcast(FP8X4), lhsT_scale=x_sc[z][:, toks],
+                        rhs=wv[:, z, cols].bitcast(FP8X4), rhs_scale=wv_sc[:, z, cols],
+                        start=(z == 0), stop=(z == 1),
+                    )
+            vb = sb.tile([P, len(rows), w], F32, name=f"vb_{name}")
+            nc.vector.scalar_tensor_tensor(
+                out=vb[:], in0=bank[:], scalar=SHARE,
+                in1=b_rows[:, cols].unsqueeze(1).to_broadcast([P, len(rows), w]),
+                op0=ALU.mult, op1=ALU.add,
+            )
+            return vb
+
+        def values_turned(q):
+            cols = slice(H + q * P, H + (q + 1) * P)
+            bank = ps.tile([P, T], F32, tag=f"v{2 + q}", name=f"val_t{q}")
+            for z in range(2):
+                nc.tensor.matmul_mx(
+                    out=bank[:], lhsT=wv[:, z, cols].bitcast(FP8X4), lhsT_scale=wv_sc[:, z, cols],
+                    rhs=x_codes[z][:].bitcast(FP8X4), rhs_scale=x_sc[z][:], start=(z == 0), stop=(z == 1),
                 )
+            vbt = sb.tile([P, T], F32, name=f"vbt{q}")
+            nc.scalar.activation(out=vbt[:], in_=bank[:], func=ACT.Identity, scale=SHARE, bias=b_part[:, q : q + 1])
+            return vbt
 
-        def products(c, vec_cols):
-            c0, w = CHUNKS[c]
-            y[c] = sb.tile([P, PACK, w], F32, name=f"y{c}")
-            yg[c] = sb.tile([P, w, PACK], BF16, align_bytes=64, name=f"yg{c}")
+        def turn_back(vbt, q):
+            bank = ps.tile([P, PACK, P], F32, tag=f"a{q}", name=f"vb_back{q}")
             for r in range(PACK):
+                nc.tensor.transpose(bank[:, r, :], vbt[:, r * P : (r + 1) * P], ident[:])
+            return bank
+
+        def products(vb, rows, cols):
+            for i, r in enumerate(rows):
                 nc.vector.scalar_tensor_tensor(
-                    out=y[c][:, r, :], in0=e[r][:, c0 : c0 + w], scalar=inv[:, r : r + 1], in1=vb[c][:, r, :],
+                    out=y[:, r, cols], in0=vb[:, i, :], scalar=inv[:, r : r + 1], in1=e[:, r, cols],
                     op0=ALU.mult, op1=ALU.mult,
                 )
-            nc.sync.dma_start(out=y_rows[:, :, c0 : c0 + w], in_=y[c][:])
-            nc.scalar.copy(
-                out=yg[c][:, vec_cols:, :].rearrange("p (c i) r -> p c r i", i=PACK),
-                in_=y[c][:, :, vec_cols:].rearrange("p r (c i) -> p c r i", i=PACK),
+            nc.sync.dma_start(out=y_rows[:, rows[0] : rows[-1] + 1, cols], in_=y[:, rows[0] : rows[-1] + 1, cols])
+
+        yg = [sb.tile([P, H, PACK], BF16, align_bytes=64, name=f"yg{h}") for h in range(2)]
+
+        def rounded(copy, h, c0, c1):
+            copy(
+                out=yg[h][:, c0:c1, :].rearrange("p (c i) r -> p c r i", i=PACK),
+                in_=y[:, :, h * H + c0 : h * H + c1].rearrange("p r (c i) -> p c r i", i=PACK),
             )
 
-        def planes(c):
-            c0, w = CHUNKS[c]
-            words = sb.tile([P, w], U32, align_bytes=64, name=f"words{c}")
+        def planes(h):
+            words = sb.tile([P, H], U32, align_bytes=64, name=f"words{h}")
             nc.vector.quantize_mx(
-                out=words[:].bitcast(FP8X4), scales=y_sc[:, c0 : c0 + w], in_=yg[c][:].rearrange("p c r -> p (c r)")
+                out=words[:].bitcast(FP8X4), scales=y_sc[:, h * H : (h + 1) * H],
+                in_=yg[h][:].rearrange("p c r -> p (c r)"),
             )
-            nc.sync.dma_start(out=word_rows[:, c0 : c0 + w], in_=words[:].bitcast(I32))
+            nc.sync.dma_start(out=word_rows[:, h * H : (h + 1) * H], in_=words[:].bitcast(I32))
 
-        values(0)
+        lo = slice(0, H)
+        vb0 = values("v0", (0, 1), lo)
+        vb1 = values("v1", (2, 3), lo)
         nc.vector.reciprocal(out=inv[:], in_=sums[:])
-        values(1)
-        products(0, 0)
-        values(2)
-        products(1, 0)
+        vbt = [values_turned(q) for q in range(2)]
+        back = [turn_back(vbt[q], q) for q in range(2)]
+        products(vb0, (0, 1), lo)
+        products(vb1, (2, 3), lo)
+        rounded(nc.scalar.copy, 0, 0, H)
+        products(back[0], (0, 1, 2, 3), slice(H, H + P))
+        rounded(nc.scalar.copy, 1, 0, P)
+        products(back[1], (0, 1, 2, 3), slice(H + P, N))
         planes(0)
-        products(2, VEC_COLS_LAST)
+        rounded(nc.vector.tensor_copy, 1, P, H)
         planes(1)
-        nc.vector.tensor_copy(
-            out=yg[2][:, :VEC_COLS_LAST, :].rearrange("p (c i) r -> p c r i", i=PACK),
-            in_=y[2][:, :, :VEC_COLS_LAST].rearrange("p r (c i) -> p c r i", i=PACK),
-        )
-        planes(2)
         for q in range(QUADS):
             queue = nc.scalar if q % 2 else nc.sync
             queue.dma_start(

@@ -74,7 +74,7 @@ def tile_mix_features_share_a_gate_pl_kernel(
         x0_raw = sb.tile([P, PACK, T], F32, align_bytes=64)
         x1_raw = [sb.tile([P, 2, T], F32, align_bytes=64, name=f"x1_raw{h}") for h in range(2)]
         ws = sb.tile([P, 2 * N], U8, align_bytes=64)
-        wa = sb.tile([P, 2, 2 * N], U8, align_bytes=64)
+        wa = [sb.tile([P, 2 * N], U8, align_bytes=64, name=f"wa{z}") for z in range(2)]
         wv = sb.tile([P, 2, N], U32, align_bytes=64)
         xt_rows = xt.rearrange("(z p j) t -> z p j t", p=P, j=PACK)
 
@@ -86,7 +86,8 @@ def tile_mix_features_share_a_gate_pl_kernel(
         nc.sync.dma_start(out=x1_raw[0][:], in_=xt_rows[1][:, 0:2, :])
         nc.sync.dma_start(out=x1_raw[1][:], in_=xt_rows[1][:, 2:4, :])
         load_scales(nc.sync, wa_sc, wa_scales)
-        nc.sync.dma_start(out=wa[:].bitcast(I32), in_=wa_words.rearrange("z p b -> p z b").bitcast(I32))
+        for z in range(2):
+            nc.sync.dma_start(out=wa[z][:].bitcast(I32), in_=wa_words[z].bitcast(I32))
         nc.sync.dma_start(out=wv[:].bitcast(I32), in_=wv_words.rearrange("z p n t -> p z (n t)").bitcast(I32))
         load_scales(nc.sync, wv_sc, wv_scales)
 
@@ -136,9 +137,19 @@ def tile_mix_features_share_a_gate_pl_kernel(
             toks = slice(r * P, (r + 1) * P)
             nc.tensor.matmul_mx(
                 out=gate[r][:], lhsT=x_codes[z][:, toks].bitcast(FP8X4), lhsT_scale=x_sc[z][:, toks],
-                rhs=wa[:, z, :].bitcast(FP4X4), rhs_scale=wa_sc[:, z, :], start=False, stop=(z == 1),
+                rhs=wa[z][:].bitcast(FP4X4), rhs_scale=wa_sc[:, z, :], start=False, stop=(z == 1),
             )
 
+        spare = ps.tile([P, BANK], F32, tag="v0")
+
+        def keep_warm(count):
+            for i in range(count):
+                nc.tensor.matmul_mx(
+                    out=spare[:], lhsT=xq_raw[:, 0:P].bitcast(FP8X4), lhsT_scale=xq_sc_raw[:, 0, 0:P],
+                    rhs=xq_raw[:].bitcast(FP8X4), rhs_scale=xq_sc_raw[:, 0, :], start=True, stop=True,
+                )
+
+        keep_warm(3)
         for r in range(PACK):
             toks = slice(r * P, (r + 1) * P)
             nc.tensor.matmul_mx(
@@ -150,6 +161,7 @@ def tile_mix_features_share_a_gate_pl_kernel(
             nc.tensor.transpose(col_bank[:, q, :], b_rows[:, H + q * P : H + (q + 1) * P], ident[:])
         b_part = sb.tile([P, 2], F32)
         nc.scalar.copy(out=b_part[:], in_=col_bank[:, :, 0])
+        keep_warm(3)
         for r, z in ((0, 0), (1, 0), (0, 1), (1, 1), (2, 0), (2, 1), (3, 0), (3, 1)):
             gate_pass(r, z)
 
@@ -224,18 +236,21 @@ def tile_mix_features_share_a_gate_pl_kernel(
                 in_=y[:, :, h * H + c0 : h * H + c1].rearrange("p r (c i) -> p c r i", i=PACK),
             )
 
-        def planes(h):
-            words = sb.tile([P, H], U32, align_bytes=64, name=f"words{h}")
+        words = [sb.tile([P, H], U32, align_bytes=64, name=f"words{h}") for h in range(2)]
+
+        def planes(h, c0, c1):
             nc.vector.quantize_mx(
-                out=words[:].bitcast(FP8X4), scales=y_sc[:, h * H : (h + 1) * H],
-                in_=yg[h][:].rearrange("p c r -> p (c r)"),
+                out=words[h][:, c0:c1].bitcast(FP8X4), scales=y_sc[:, h * H + c0 : h * H + c1],
+                in_=yg[h][:, c0:c1, :].rearrange("p c r -> p (c r)"),
             )
-            nc.sync.dma_start(out=word_rows[:, h * H : (h + 1) * H], in_=words[:].bitcast(I32))
+            if c1 == H:
+                nc.sync.dma_start(out=word_rows[:, h * H : (h + 1) * H], in_=words[h][:].bitcast(I32))
 
         lo = slice(0, H)
+        nc.vector.reciprocal(out=inv[:, 0:2], in_=sums[:, 0:2])
         vb0 = values("v0", (0, 1), lo)
         vb1 = values("v1", (2, 3), lo)
-        nc.vector.reciprocal(out=inv[:], in_=sums[:])
+        nc.vector.reciprocal(out=inv[:, 2:4], in_=sums[:, 2:4])
         vbt = [values_turned(q) for q in range(2)]
         back = [turn_back(vbt[q], q) for q in range(2)]
         products(vb0, (0, 1), lo)
@@ -244,9 +259,10 @@ def tile_mix_features_share_a_gate_pl_kernel(
         products(back[0], (0, 1, 2, 3), slice(H, H + P))
         rounded(nc.scalar.copy, 1, 0, P)
         products(back[1], (0, 1, 2, 3), slice(H + P, N))
-        planes(0)
+        planes(0, 0, H)
         rounded(nc.vector.tensor_copy, 1, P, H)
-        planes(1)
+        planes(1, 0, P)
+        planes(1, P, H)
         for q in range(QUADS):
             queue = nc.scalar if q % 2 else nc.sync
             queue.dma_start(

@@ -40,10 +40,10 @@ def load_scales(queue, plane, scales):
 
 def deal_and_round(nc, grouped, raw, vec_m):
     count = grouped.shape[2]
-    dst = grouped.rearrange("p r m j -> p m j r")
-    src = raw.rearrange("p j (m r) -> p m j r", r=PACK)
-    nc.vector.tensor_copy(out=dst[:, :vec_m], in_=src[:, :vec_m])
-    nc.scalar.copy(out=dst[:, vec_m:count], in_=src[:, vec_m:count])
+    dst = grouped.rearrange("p r (b m) j -> p b j m r", m=2)
+    src = raw.rearrange("p j (b m r) -> p b j m r", m=2, r=PACK)
+    nc.vector.tensor_copy(out=dst[:, : vec_m // 2], in_=src[:, : vec_m // 2])
+    nc.scalar.copy(out=dst[:, vec_m // 2 : count // 2], in_=src[:, vec_m // 2 : count // 2])
 
 
 def tile_mix_features_share_a_gate_pl_kernel(
@@ -94,11 +94,12 @@ def tile_mix_features_share_a_gate_pl_kernel(
         xq = sb.tile([P, T], I32, align_bytes=64)
         xq_sc = sb.tile([P, T], U8, align_bytes=64)
         nc.vector.tensor_copy(
-            out=xq[:].rearrange("p (r m) -> p m r", r=PACK), in_=xq_raw[:].rearrange("p (m r) -> p m r", r=PACK)
+            out=xq[:].rearrange("p (r b m) -> p b r m", r=PACK, m=4),
+            in_=xq_raw[:].rearrange("p (b m r) -> p b r m", r=PACK, m=4),
         )
         nc.vector.tensor_copy(
-            out=xq_sc[:].rearrange("p (r m) -> p m r", r=PACK),
-            in_=xq_sc_raw[:, 0, :].rearrange("p (m r) -> p m r", r=PACK),
+            out=xq_sc[:].rearrange("p (r b m) -> p b r m", r=PACK, m=16),
+            in_=xq_sc_raw[:, 0, :].rearrange("p (b m r) -> p b r m", r=PACK, m=16),
         )
 
         b_bank = ps.tile([P, PACK, P], F32, tag="v3")
@@ -140,16 +141,6 @@ def tile_mix_features_share_a_gate_pl_kernel(
                 rhs=wa[z][:].bitcast(FP4X4), rhs_scale=wa_sc[:, z, :], start=False, stop=(z == 1),
             )
 
-        spare = ps.tile([P, BANK], F32, tag="v0")
-
-        def keep_warm(count):
-            for i in range(count):
-                nc.tensor.matmul_mx(
-                    out=spare[:], lhsT=xq_raw[:, 0:P].bitcast(FP8X4), lhsT_scale=xq_sc_raw[:, 0, 0:P],
-                    rhs=xq_raw[:].bitcast(FP8X4), rhs_scale=xq_sc_raw[:, 0, :], start=True, stop=True,
-                )
-
-        keep_warm(3)
         for r in range(PACK):
             toks = slice(r * P, (r + 1) * P)
             nc.tensor.matmul_mx(
@@ -161,7 +152,6 @@ def tile_mix_features_share_a_gate_pl_kernel(
             nc.tensor.transpose(col_bank[:, q, :], b_rows[:, H + q * P : H + (q + 1) * P], ident[:])
         b_part = sb.tile([P, 2], F32)
         nc.scalar.copy(out=b_part[:], in_=col_bank[:, :, 0])
-        keep_warm(3)
         for r, z in ((0, 0), (1, 0), (0, 1), (1, 1), (2, 0), (2, 1), (3, 0), (3, 1)):
             gate_pass(r, z)
 

@@ -26,7 +26,7 @@ SHARE = 512.0
 
 CHUNKS = ((0, 256), (256, 128), (384, 128))
 VEC_M_PASS0 = 80
-VEC_M_HALF = (72, 84)
+VEC_M_HALF = (28, 40)
 VEC_COLS_LAST = 224
 
 
@@ -72,7 +72,7 @@ def tile_mix_features_share_a_gate_pl_kernel(
 
         xq_raw = sb.tile([P, T], I32, align_bytes=64)
         x0_raw = sb.tile([P, PACK, T], F32, align_bytes=64)
-        x1_raw = [sb.tile([P, 2, T], F32, align_bytes=64, name=f"x1_raw{h}") for h in range(2)]
+        x1_raw = [sb.tile([P, PACK, HALF], F32, align_bytes=64, name=f"x1_raw{h}") for h in range(2)]
         ws = sb.tile([P, 2 * N], U8, align_bytes=64)
         wa = [sb.tile([P, 2 * N], U8, align_bytes=64, name=f"wa{z}") for z in range(2)]
         wv = sb.tile([P, 2, N], U32, align_bytes=64)
@@ -83,8 +83,8 @@ def tile_mix_features_share_a_gate_pl_kernel(
         load_scales(nc.sync, xq_sc_raw, xq_scales)
         nc.sync.dma_start(out=x0_raw[:], in_=xt_rows[0])
         load_scales(nc.sync, ws_sc, ws_scales)
-        nc.sync.dma_start(out=x1_raw[0][:], in_=xt_rows[1][:, 0:2, :])
-        nc.sync.dma_start(out=x1_raw[1][:], in_=xt_rows[1][:, 2:4, :])
+        nc.sync.dma_start(out=x1_raw[0][:], in_=xt_rows[1][:, :, :HALF])
+        nc.sync.dma_start(out=x1_raw[1][:], in_=xt_rows[1][:, :, HALF:])
         load_scales(nc.sync, wa_sc, wa_scales)
         for z in range(2):
             nc.sync.dma_start(out=wa[z][:].bitcast(I32), in_=wa_words[z].bitcast(I32))
@@ -113,6 +113,11 @@ def tile_mix_features_share_a_gate_pl_kernel(
         )
 
         H = N // 2
+        col_bank = ps.tile([P, 2, P], F32, tag="v2")
+        for q in range(2):
+            nc.tensor.transpose(col_bank[:, q, :], b_rows[:, H + q * P : H + (q + 1) * P], ident[:])
+        b_part = sb.tile([P, 2], F32)
+        nc.vector.tensor_copy(out=b_part[:], in_=col_bank[:, :, 0])
 
         x_codes = [sb.tile([P, T], U32, align_bytes=64, name=f"x_codes{z}") for z in range(2)]
         x_sc = [sb.tile([P, T], U8, align_bytes=64, name=f"x_sc{z}") for z in range(2)]
@@ -121,16 +126,23 @@ def tile_mix_features_share_a_gate_pl_kernel(
         nc.vector.quantize_mx(
             out=x_codes[0][:].bitcast(FP8X4), scales=x_sc[0][:], in_=g0[:].rearrange("p r m j -> p (r m j)")
         )
-        g1 = sb.tile([P, PACK, P, PACK], BF16, align_bytes=64)
-        for h in range(2):
-            deal_and_round(nc, g1[:, :, :, 2 * h : 2 * h + 2], x1_raw[h][:], VEC_M_HALF[h])
-        for r in range(0, PACK, 2):
-            cols = slice(r * P, (r + 2) * P)
+        g1 = [sb.tile([P, PACK, P // 2, PACK], BF16, align_bytes=64, name=f"g1{h}") for h in range(2)]
+
+        def quantize_half(h, r):
+            cols = slice(r * P + h * P // 2, r * P + (h + 1) * P // 2)
             nc.vector.quantize_mx(
                 out=x_codes[1][:, cols].bitcast(FP8X4),
                 scales=x_sc[1][:, cols],
-                in_=g1[:, r : r + 2].rearrange("p r m j -> p (r m j)"),
+                in_=g1[h][:, r].rearrange("p m j -> p (m j)"),
             )
+
+        deal_and_round(nc, g1[0][:], x1_raw[0][:], VEC_M_HALF[0])
+        for r in range(PACK - 1):
+            quantize_half(0, r)
+        deal_and_round(nc, g1[1][:], x1_raw[1][:], VEC_M_HALF[1])
+        quantize_half(0, PACK - 1)
+        for r in range(PACK):
+            quantize_half(1, r)
 
         gate = [ps.tile([P, BANK], F32, tag=f"a{r}", name=f"gate{r}") for r in range(PACK)]
 
@@ -147,13 +159,9 @@ def tile_mix_features_share_a_gate_pl_kernel(
                 out=gate[r][:], lhsT=xq[:, toks].bitcast(FP8X4), lhsT_scale=xq_sc[:, toks],
                 rhs=ws[:].bitcast(FP4X4), rhs_scale=ws_sc[:, 0, :], start=True, stop=False,
             )
-        col_bank = ps.tile([P, 2, P], F32, tag="v2")
-        for q in range(2):
-            nc.tensor.transpose(col_bank[:, q, :], b_rows[:, H + q * P : H + (q + 1) * P], ident[:])
-        b_part = sb.tile([P, 2], F32)
-        nc.scalar.copy(out=b_part[:], in_=col_bank[:, :, 0])
-        for r, z in ((0, 0), (1, 0), (0, 1), (1, 1), (2, 0), (2, 1), (3, 0), (3, 1)):
-            gate_pass(r, z)
+        for r in range(PACK):
+            for z in range(2):
+                gate_pass(r, z)
 
         neg_max = sb.tile([P, PACK], F32)
         sums = sb.tile([P, PACK], F32)

from contextlib import ExitStack

import concourse.mybir as mybir
from concourse.masks import make_identity

K, L, T, N = 1024, 512, 512, 512
FLOPS = 2 * T * N * (K + L + K)

F32 = mybir.dt.float32
BF16 = mybir.dt.bfloat16
I32 = mybir.dt.int32
U32 = mybir.dt.uint32
U8 = mybir.dt.uint8
FP8X4 = mybir.dt.float8_e4m3fn_x4
FP4X4 = mybir.dt.float4_e2m1fn_x4
ALU = mybir.AluOpType
ACT = mybir.ActivationFunctionType

P = 128
PACK = 4
K_PASS = P * PACK
BANK = 512
QUADS = 4
HALF = T // 2
SHARE = 512.0

CHUNKS = ((0, 256), (256, 128), (384, 128))
VEC_M_PASS0 = 80
VEC_M_HALF = (28, 40)
VEC_COLS_LAST = 224


def load_scales(queue, plane, scales):
    for q in range(QUADS):
        queue.dma_start(
            out=plane[32 * q : 32 * q + 4, :, :].bitcast(I32),
            in_=scales[:, 4 * q : 4 * q + 4, :].rearrange("z q n -> q z n").bitcast(I32),
        )


def deal_and_round(nc, grouped, raw, vec_m):
    count = grouped.shape[2]
    dst = grouped.rearrange("p r (b m) j -> p b j m r", m=2)
    src = raw.rearrange("p j (b m r) -> p b j m r", m=2, r=PACK)
    nc.vector.tensor_copy(out=dst[:, : vec_m // 2], in_=src[:, : vec_m // 2])
    nc.scalar.copy(out=dst[:, vec_m // 2 : count // 2], in_=src[:, vec_m // 2 : count // 2])


def tile_mix_features_share_a_gate_pl_kernel(
    tc, xt, wa_words, wa_scales, xq_words, xq_scales, ws_words, ws_scales, wv_words, wv_scales, bi,
    out_0, out_1, out_2,
):
    nc = tc.nc
    with ExitStack() as ctx:
        sb = ctx.enter_context(tc.tile_pool(name="sb", bufs=1))
        ps = ctx.enter_context(tc.psum_pool(name="ps", bufs=1))
        ctx.enter_context(tc.manual_schedule())

        xq_sc_raw = sb.tile([P, 1, T], U8, align_bytes=64)
        ws_sc = sb.tile([P, 1, N], U8, align_bytes=64)
        wa_sc = sb.tile([P, 2, N], U8, align_bytes=64)
        wv_sc = sb.tile([P, 2, N], U8, align_bytes=64)
        nc.gpsimd.memset(xq_sc_raw[:].bitcast(U32), 0)
        for plane in (ws_sc, wa_sc, wv_sc):
            nc.vector.memset(plane[:].bitcast(U32), 0)

        b_cols = sb.tile([P, PACK], F32)
        nc.scalar.dma_start(out=b_cols[:], in_=bi.rearrange("o (k j) -> k (o j)", j=PACK))

        ident = sb.tile([P, P], F32)
        make_identity(nc, ident[:])

        xq_raw = sb.tile([P, T], I32, align_bytes=64)
        x0_raw = sb.tile([P, PACK, T], F32, align_bytes=64)
        x1_raw = [sb.tile([P, PACK, HALF], F32, align_bytes=64, name=f"x1_raw{h}") for h in range(2)]
        ws = sb.tile([P, 2 * N], U8, align_bytes=64)
        wa = [sb.tile([P, 2 * N], U8, align_bytes=64, name=f"wa{z}") for z in range(2)]
        wv = sb.tile([P, 2, N], U32, align_bytes=64)
        xt_rows = xt.rearrange("(z p j) t -> z p j t", p=P, j=PACK)

        nc.sync.dma_start(out=xq_raw[:], in_=xq_words.rearrange("z p c t -> p (z c t)").bitcast(I32))
        nc.sync.dma_start(out=ws[:].bitcast(I32), in_=ws_words.rearrange("z p b -> p (z b)").bitcast(I32))
        load_scales(nc.sync, xq_sc_raw, xq_scales)
        nc.sync.dma_start(out=x0_raw[:], in_=xt_rows[0])
        load_scales(nc.sync, ws_sc, ws_scales)
        nc.sync.dma_start(out=x1_raw[0][:], in_=xt_rows[1][:, :, :HALF])
        nc.sync.dma_start(out=x1_raw[1][:], in_=xt_rows[1][:, :, HALF:])
        load_scales(nc.sync, wa_sc, wa_scales)
        for z in range(2):
            nc.sync.dma_start(out=wa[z][:].bitcast(I32), in_=wa_words[z].bitcast(I32))
        nc.sync.dma_start(out=wv[:].bitcast(I32), in_=wv_words.rearrange("z p n t -> p z (n t)").bitcast(I32))
        load_scales(nc.sync, wv_sc, wv_scales)

        xq = sb.tile([P, T], I32, align_bytes=64)
        xq_sc = sb.tile([P, T], U8, align_bytes=64)
        nc.vector.tensor_copy(
            out=xq[:].rearrange("p (r b m) -> p b r m", r=PACK, m=4),
            in_=xq_raw[:].rearrange("p (b m r) -> p b r m", r=PACK, m=4),
        )
        nc.vector.tensor_copy(
            out=xq_sc[:].rearrange("p (r b m) -> p b r m", r=PACK, m=16),
            in_=xq_sc_raw[:, 0, :].rearrange("p (b m r) -> p b r m", r=PACK, m=16),
        )

        b_bank = ps.tile([P, PACK, P], F32, tag="v3")
        for j in range(PACK):
            nc.tensor.transpose(b_bank[:, j, :], b_cols[:, j : j + 1].to_broadcast([P, P]), ident[:])
        b_rows = sb.tile([P, N], F32)
        nc.scalar.activation(
            out=b_rows[:].rearrange("p (k j) -> p k j", j=PACK),
            in_=b_bank[:].rearrange("p j k -> p k j"),
            func=ACT.Copy, scale=SHARE,
        )

        H = N // 2
        col_bank = ps.tile([P, 2, P], F32, tag="v2")
        for q in range(2):
            nc.tensor.transpose(col_bank[:, q, :], b_rows[:, H + q * P : H + (q + 1) * P], ident[:])
        b_part = sb.tile([P, 2], F32)
        nc.vector.tensor_copy(out=b_part[:], in_=col_bank[:, :, 0])

        x_codes = [sb.tile([P, T], U32, align_bytes=64, name=f"x_codes{z}") for z in range(2)]
        x_sc = [sb.tile([P, T], U8, align_bytes=64, name=f"x_sc{z}") for z in range(2)]
        g0 = sb.tile([P, PACK, P, PACK], BF16, align_bytes=64)
        deal_and_round(nc, g0[:], x0_raw[:], VEC_M_PASS0)
        nc.vector.quantize_mx(
            out=x_codes[0][:].bitcast(FP8X4), scales=x_sc[0][:], in_=g0[:].rearrange("p r m j -> p (r m j)")
        )
        g1 = [sb.tile([P, PACK, P // 2, PACK], BF16, align_bytes=64, name=f"g1{h}") for h in range(2)]

        def quantize_half(h, r):
            cols = slice(r * P + h * P // 2, r * P + (h + 1) * P // 2)
            nc.vector.quantize_mx(
                out=x_codes[1][:, cols].bitcast(FP8X4),
                scales=x_sc[1][:, cols],
                in_=g1[h][:, r].rearrange("p m j -> p (m j)"),
            )

        deal_and_round(nc, g1[0][:], x1_raw[0][:], VEC_M_HALF[0])
        for r in range(PACK - 1):
            quantize_half(0, r)
        deal_and_round(nc, g1[1][:], x1_raw[1][:], VEC_M_HALF[1])
        quantize_half(0, PACK - 1)
        for r in range(PACK):
            quantize_half(1, r)

        gate = [ps.tile([P, BANK], F32, tag=f"a{r}", name=f"gate{r}") for r in range(PACK)]

        def gate_pass(r, z):
            toks = slice(r * P, (r + 1) * P)
            nc.tensor.matmul_mx(
                out=gate[r][:], lhsT=x_codes[z][:, toks].bitcast(FP8X4), lhsT_scale=x_sc[z][:, toks],
                rhs=wa[z][:].bitcast(FP4X4), rhs_scale=wa_sc[:, z, :], start=False, stop=(z == 1),
            )

        for r in range(PACK):
            toks = slice(r * P, (r + 1) * P)
            nc.tensor.matmul_mx(
                out=gate[r][:], lhsT=xq[:, toks].bitcast(FP8X4), lhsT_scale=xq_sc[:, toks],
                rhs=ws[:].bitcast(FP4X4), rhs_scale=ws_sc[:, 0, :], start=True, stop=False,
            )
        for r in range(PACK):
            for z in range(2):
                gate_pass(r, z)

        neg_max = sb.tile([P, PACK], F32)
        sums = sb.tile([P, PACK], F32)
        inv = sb.tile([P, PACK], F32)
        e = sb.tile([P, PACK, N], F32)
        for r in range(PACK):
            nc.vector.tensor_reduce(
                out=neg_max[:, r : r + 1], in_=gate[r][:], axis=mybir.AxisListType.X, op=ALU.max, negate=True
            )
            nc.scalar.activation(
                out=e[:, r, :], in_=gate[r][:], func=ACT.Exp, bias=neg_max[:, r : r + 1], scale=1.0,
                accum_out=sums[:, r : r + 1],
            )

        y_rows = out_0.rearrange("(p r) n -> p r n", r=PACK)
        word_rows = out_1.rearrange("z p c t -> p (z c t)").bitcast(I32)
        y_sc = sb.tile([P, N], U8, align_bytes=64)
        y = sb.tile([P, PACK, N], F32)

        def values(name, rows, cols):
            w = cols.stop - cols.start
            bank = ps.tile([P, len(rows), w], F32, tag=name, name=f"val_{name}")
            for i, r in enumerate(rows):
                toks = slice(r * P, (r + 1) * P)
                for z in range(2):
                    nc.tensor.matmul_mx(
                        out=bank[:, i, :], lhsT=x_codes[z][:, toks].bitcast(FP8X4), lhsT_scale=x_sc[z][:, toks],
                        rhs=wv[:, z, cols].bitcast(FP8X4), rhs_scale=wv_sc[:, z, cols],
                        start=(z == 0), stop=(z == 1),
                    )
            vb = sb.tile([P, len(rows), w], F32, name=f"vb_{name}")
            nc.vector.scalar_tensor_tensor(
                out=vb[:], in0=bank[:], scalar=SHARE,
                in1=b_rows[:, cols].unsqueeze(1).to_broadcast([P, len(rows), w]),
                op0=ALU.mult, op1=ALU.add,
            )
            return vb

        def values_turned(q):
            cols = slice(H + q * P, H + (q + 1) * P)
            bank = ps.tile([P, T], F32, tag=f"v{2 + q}", name=f"val_t{q}")
            for z in range(2):
                nc.tensor.matmul_mx(
                    out=bank[:], lhsT=wv[:, z, cols].bitcast(FP8X4), lhsT_scale=wv_sc[:, z, cols],
                    rhs=x_codes[z][:].bitcast(FP8X4), rhs_scale=x_sc[z][:], start=(z == 0), stop=(z == 1),
                )
            vbt = sb.tile([P, T], F32, name=f"vbt{q}")
            nc.scalar.activation(out=vbt[:], in_=bank[:], func=ACT.Identity, scale=SHARE, bias=b_part[:, q : q + 1])
            return vbt

        def turn_back(vbt, q):
            bank = ps.tile([P, PACK, P], F32, tag=f"a{q}", name=f"vb_back{q}")
            for r in range(PACK):
                nc.tensor.transpose(bank[:, r, :], vbt[:, r * P : (r + 1) * P], ident[:])
            return bank

        def products(vb, rows, cols):
            for i, r in enumerate(rows):
                nc.vector.scalar_tensor_tensor(
                    out=y[:, r, cols], in0=vb[:, i, :], scalar=inv[:, r : r + 1], in1=e[:, r, cols],
                    op0=ALU.mult, op1=ALU.mult,
                )
            nc.sync.dma_start(out=y_rows[:, rows[0] : rows[-1] + 1, cols], in_=y[:, rows[0] : rows[-1] + 1, cols])

        yg = [sb.tile([P, H, PACK], BF16, align_bytes=64, name=f"yg{h}") for h in range(2)]

        def rounded(copy, h, c0, c1):
            copy(
                out=yg[h][:, c0:c1, :].rearrange("p (c i) r -> p c r i", i=PACK),
                in_=y[:, :, h * H + c0 : h * H + c1].rearrange("p r (c i) -> p c r i", i=PACK),
            )

        words = [sb.tile([P, H], U32, align_bytes=64, name=f"words{h}") for h in range(2)]

        def planes(h, c0, c1):
            nc.vector.quantize_mx(
                out=words[h][:, c0:c1].bitcast(FP8X4), scales=y_sc[:, h * H + c0 : h * H + c1],
                in_=yg[h][:, c0:c1, :].rearrange("p c r -> p (c r)"),
            )
            if c1 == H:
                nc.sync.dma_start(out=word_rows[:, h * H : (h + 1) * H], in_=words[h][:].bitcast(I32))

        lo = slice(0, H)
        nc.vector.reciprocal(out=inv[:, 0:2], in_=sums[:, 0:2])
        vb0 = values("v0", (0, 1), lo)
        vb1 = values("v1", (2, 3), lo)
        nc.vector.reciprocal(out=inv[:, 2:4], in_=sums[:, 2:4])
        vbt = [values_turned(q) for q in range(2)]
        back = [turn_back(vbt[q], q) for q in range(2)]
        products(vb0, (0, 1), lo)
        products(vb1, (2, 3), lo)
        rounded(nc.scalar.copy, 0, 0, H)
        products(back[0], (0, 1, 2, 3), slice(H, H + P))
        rounded(nc.scalar.copy, 1, 0, P)
        products(back[1], (0, 1, 2, 3), slice(H + P, N))
        planes(0, 0, H)
        rounded(nc.vector.tensor_copy, 1, P, H)
        planes(1, 0, P)
        planes(1, P, H)
        for q in range(QUADS):
            queue = nc.scalar if q % 2 else nc.sync
            queue.dma_start(
                out=out_2[0, 4 * q : 4 * q + 4, :].bitcast(I32), in_=y_sc[32 * q : 32 * q + 4, :].bitcast(I32)
            )
